import numpy as np
import ml_dtypes


def mxq(x, axis, fmt="e4m3"):
    dtype, down = {"e4m3": (ml_dtypes.float8_e4m3fn, 7), "e5m2": (ml_dtypes.float8_e5m2, 14)}[fmt]
    v = np.moveaxis(np.asarray(x, np.float32).astype(ml_dtypes.bfloat16).astype(np.float64), axis, -1)
    blocks = v.reshape(v.shape[:-1] + (-1, 32))
    amax = np.abs(blocks).max(-1, keepdims=True)
    byte = np.maximum(np.where(amax > 0, np.frexp(amax)[1] - 1 + 127, 0) - down, 1)
    scale = np.exp2(byte - 127.0)
    codes = (blocks / scale).astype(np.float32).astype(dtype).astype(np.float64)
    return np.moveaxis((codes * scale).reshape(v.shape), -1, axis)


WIDE = False


def mx_kscale(k):
    if not WIDE:
        return np.ones(k)
    levels = np.array([10, -10, 5, -5, 0])
    if k % 512:
        return np.exp2(np.random.permutation(np.resize(levels, k // 32))).repeat(32)
    a = np.empty((k // 512, 16))
    for p in range(k // 512):
        a[p, :8] = np.random.permutation(np.resize(levels, 8))
        for g in range(8):
            far = levels[np.abs(levels - a[p, g]) >= 10]
            a[p, g + 8] = far[np.random.randint(len(far))]
    return np.exp2(a.ravel()).repeat(32)


def f64(x):
    return np.asarray(x).astype(np.float64)


def striped(idx):
    return np.tile(idx.reshape(-1, 16).T, (8, 1)).astype(np.uint16)


def unstriped(offs):
    return offs[:16].T.reshape(-1).astype(np.int64)


def striped8(idx):
    return np.concatenate([x.reshape(-1, 16).T for x in idx]).astype(np.uint16)


def runs(offs, k):
    lists = np.stack([offs[16 * r : 16 * r + 16].T.reshape(-1) for r in range(8)]).astype(np.int64)
    return lists[np.arange(k) % 512 // 64]


def pack_weight(w):
    k, n = w.shape
    w = f64(np.asarray(w, np.float32).astype(ml_dtypes.bfloat16)).reshape(k // 32, 32, n)
    amax = np.abs(w).max(1)
    byte = np.clip(np.where(amax > 0, np.frexp(amax)[1] - 1 + 127 - 7, 1), 1, 254)
    scaled = (w * np.exp2(127.0 - byte)[:, None, :]).reshape(k, n).astype(np.float32)
    words = np.ascontiguousarray(scaled.reshape(k // 512, 128, 4, n).transpose(0, 1, 3, 2)).astype(ml_dtypes.float8_e4m3fn).view(np.uint8)
    return words, np.ascontiguousarray(byte.astype(np.uint8).reshape(k // 512, 16, n))


def unpack_weight(words, scales):
    g, p, n, _ = words.shape
    vals = np.ascontiguousarray(words).view(ml_dtypes.float8_e4m3fn).astype(np.float64) * np.repeat(np.exp2(scales.astype(np.float64) - 127.0), 8, axis=1)[..., None]
    return vals.transpose(0, 1, 3, 2).reshape(g * 512, n)


K, T, S, H, C, W = 512, 2048, 512, 512, 512, 256


def setup_inputs():
    n = np.random.standard_normal
    s = mx_kscale(K)[:, None]
    packed_xT = pack_weight(n((K, T)) * s)
    perm = np.stack([np.random.permutation(S) for _ in range(8)])
    return {
        "x_words": packed_xT[0],
        "x_scales": packed_xT[1],
        "w1": (n((K, H)) / np.sqrt(K) / s).astype(np.float32),
        "gs": (np.random.uniform(0.5, 1.5, (K, 1)) / s).astype(np.float32),
        "offs": striped(np.random.permutation(T)[:S]),
        "n1": striped8(np.stack([np.random.permutation(S) for _ in range(8)])),
        "n2": striped8(np.stack([np.random.permutation(S) for _ in range(8)])),
        "cand": striped(np.random.permutation(T)[:C]),
        "n3": striped8(perm[:, :W]),
        "n4": striped8(perm[:, W:]),
        "n5": striped8(np.stack([np.random.permutation(S) for _ in range(8)])),
    }


def reference(x_words, x_scales, w1, gs, offs, n1, n2, cand, n3, n4, n5):
    x_cand = unpack_weight(x_words, x_scales)[:, unstriped(cand)]
    xq = unpack_weight(x_words, x_scales)[:, unstriped(offs)]
    y = mxq(f64(w1), 0, "e4m3").T @ xq
    z = f64(gs) * (y[np.arange(H)[:, None], runs(n1, H)] + 0.75 * (y[np.arange(H)[:, None], runs(n2, H)]))
    s = 0.0625 * ((x_cand.T @ mxq(z, 0, "e4m3")))
    pa = s[np.arange(C)[:, None], runs(n3, C)]
    pb = s[np.arange(C)[:, None], runs(n4, C)]
    ra = pa - (0.5 * pb)
    ds = s.copy()
    ds[np.arange(C)[:, None], runs(n4, C)] = ra
    return ds - (0.5 * (ds[np.arange(C)[:, None], runs(n5, C)]))

@@ -1,0 +1,181 @@
+from contextlib import ExitStack
+
+import concourse.mybir as mybir
+
+F32 = mybir.dt.float32
+BF16 = mybir.dt.bfloat16
+I32 = mybir.dt.int32
+U32 = mybir.dt.uint32
+U16 = mybir.dt.uint16
+U8 = mybir.dt.uint8
+FP8X4 = mybir.dt.float8_e4m3fn_x4
+MULT = mybir.AluOpType.mult
+ADD = mybir.AluOpType.add
+COPY = mybir.ActivationFunctionType.Copy
+
+P = 128
+PACK = 4
+T = 2048
+N = 512
+HALF = 256
+FLOPS = 2 * 2 * 512 * 512 * 512
+
+
+def cols16(lo, hi):
+    return slice(lo // 16, hi // 16)
+
+
+def tile_picked_candsumfoldd_none_p_kernel(tc, x_words, x_scales, w1, gs, offs, n1, n2, cand, n3, n4, n5, out):
+    nc = tc.nc
+    with ExitStack() as ctx:
+        keep = ctx.enter_context(tc.tile_pool(name="keep", bufs=1))
+        psum = ctx.enter_context(tc.psum_pool(name="psum", bufs=1))
+
+        def load_list(name, src):
+            tile = keep.tile(list(src.shape), U16, name=name)
+            nc.sync.dma_start(tile[:], src)
+            return tile
+
+        xs = keep.tile([P, T], U8, name="xs")
+        offs_sb = load_list("offs_sb", offs)
+        for q in range(4):
+            rows = x_scales[0, 4 * q : 4 * q + 4, :].bitcast(I32)
+            nc.sync.dma_start(xs[32 * q : 32 * q + 32, :].bitcast(I32), rows.unsqueeze(0).to_broadcast([8, 4, T // 4]))
+        cand_sb = load_list("cand_sb", cand)
+        xw = keep.tile([P, T], I32, name="xw")
+        nc.sync.dma_start(xw[:], x_words[0].rearrange("p n t -> p (n t)").bitcast(I32))
+        w_raw = keep.tile([P, PACK, N], F32, name="w_raw")
+        nc.sync.dma_start(w_raw[:], w1.rearrange("(p j) c -> p j c", j=PACK))
+        gs_sb = keep.tile([P, PACK], F32, name="gs_sb")
+        nc.sync.dma_start(gs_sb[:], gs.rearrange("(p t) o -> p (t o)", t=PACK))
+        n2_sb = load_list("n2_sb", n2)
+        n1_sb = load_list("n1_sb", n1)
+        n3_sb = load_list("n3_sb", n3)
+        n4_sb = load_list("n4_sb", n4)
+        n5_sb = load_list("n5_sb", n5)
+
+        pick_scales = keep.tile([P, N], U8, name="pick_scales", align_bytes=64)
+        nc.vector.tensor_copy(pick_scales[:], xs[:].indirect(offs_sb[:]))
+        cand_scales_raw = keep.tile([P, N], U8, name="cand_scales_raw", align_bytes=64)
+        nc.vector.tensor_copy(cand_scales_raw[:], xs[:].indirect(cand_sb[:]))
+        cand_scales = keep.tile([P, N], U8, name="cand_scales", align_bytes=64)
+        nc.vector.tensor_copy(
+            cand_scales[:].bitcast(I32).rearrange("p (t a b) -> p t a b", t=4, a=16),
+            cand_scales_raw[:].bitcast(I32).rearrange("p (a t b) -> p t a b", t=4, a=16),
+        )
+
+        pick_words = keep.tile([P, N], U32, name="pick_words", align_bytes=64)
+        nc.vector.tensor_copy(pick_words[:], xw[:].bitcast(U32).indirect(offs_sb[:]))
+        cand_words = keep.tile([P, N], U32, name="cand_words", align_bytes=64)
+        nc.vector.tensor_copy(
+            cand_words[:].rearrange("p (t a b) -> p a t b", t=4, a=16), xw[:].bitcast(U32).indirect(cand_sb[:])
+        )
+
+        w_src = w_raw[:].rearrange("p j (m u e) -> p u m j e", u=2, e=2)
+        w_codes, w_scales = [], []
+        for u in range(2):
+            w_bf = keep.tile([P, 2, P, PACK], BF16, name="w_bf%d" % u, align_bytes=64)
+            w_dst = w_bf[:].rearrange("p e m j -> p m j e")
+            if u == 0:
+                nc.vector.tensor_copy(w_dst, w_src[:, u])
+            else:
+                nc.scalar.copy(w_dst, w_src[:, u])
+            codes = keep.tile([P, HALF], U32, name="w_codes%d" % u, align_bytes=64)
+            scales = keep.tile([P, HALF], U8, name="w_scales%d" % u, align_bytes=64)
+            nc.vector.quantize_mx(out=codes[:].bitcast(FP8X4), scales=scales[:], in_=w_bf[:].rearrange("p e m j -> p (e m j)"))
+            w_codes.append(codes)
+            w_scales.append(scales)
+
+        gy = []
+        for t in range(PACK):
+            acc = psum.tile([P, N], F32, name="y_acc%d" % t)
+            m = slice(P * (t % 2), P * (t % 2 + 1))
+            nc.tensor.matmul_mx(
+                out=acc[:], lhsT=w_codes[t // 2][:, m].bitcast(FP8X4), lhsT_scale=w_scales[t // 2][:, m],
+                rhs=pick_words[:].bitcast(FP8X4), rhs_scale=pick_scales[:], start=True, stop=True,
+            )
+            g = keep.tile([P, N], F32, name="gy%d" % t)
+            nc.scalar.activation(g[:], acc[:], COPY, scale=gs_sb[:, t : t + 1])
+            gy.append(g)
+
+        z32 = keep.tile([P, PACK, N], F32, name="z32")
+        far = keep.tile([P, PACK, N], F32, name="far")
+        z_bf = keep.tile([P, N, PACK], BF16, name="z_bf", align_bytes=64)
+        z_codes = keep.tile([P, N], U32, name="z_codes", align_bytes=64)
+        z_scales = keep.tile([P, N], U8, name="z_scales", align_bytes=64)
+        halves = [(0, 256), (256, 512)]
+        pieces = [(0, 256), (256, 384), (384, 512)]
+
+        def gather_far(t, lo, hi):
+            nc.vector.tensor_scalar(far[:, t, lo:hi], gy[t][:].indirect(n2_sb[:, cols16(lo, hi)]), 0.75, 0.0, MULT, ADD)
+
+        def gather_near(t, lo, hi):
+            nc.vector.tensor_tensor(z32[:, t, lo:hi], gy[t][:].indirect(n1_sb[:, cols16(lo, hi)]), far[:, t, lo:hi], ADD)
+
+        def weave(u, lo, hi):
+            nc.scalar.copy(z_bf[:, lo:hi, 2 * u : 2 * u + 2], z32[:, 2 * u : 2 * u + 2, lo:hi].rearrange("p e j -> p j e"))
+
+        for t in range(PACK - 1):
+            for lo, hi in halves:
+                gather_far(t, lo, hi)
+            for lo, hi in halves:
+                gather_near(t, lo, hi)
+            if t == 1:
+                weave(0, 0, N)
+        for lo, hi in halves:
+            gather_far(3, lo, hi)
+        s_acc = [psum.tile([P, N], F32, name="s_acc%d" % t) for t in range(PACK)]
+        s = [keep.tile([P, N], F32, name="s%d" % t) for t in range(PACK)]
+        ds = [keep.tile([P, N], F32, name="ds%d" % t) for t in range(PACK)]
+        for lo, hi in pieces:
+            gather_near(3, lo, hi)
+            weave(1, lo, hi)
+        for lo, hi in pieces:
+            nc.vector.quantize_mx(
+                out=z_codes[:, lo:hi].bitcast(FP8X4), scales=z_scales[:, lo:hi],
+                in_=z_bf[:, lo:hi, :].rearrange("p j t -> p (j t)"),
+            )
+            for t in range(PACK):
+                m = slice(P * t, P * (t + 1))
+                nc.tensor.matmul_mx(
+                    out=s_acc[t][:, lo:hi], lhsT=cand_words[:, m].bitcast(FP8X4), lhsT_scale=cand_scales[:, m],
+                    rhs=z_codes[:, lo:hi].bitcast(FP8X4), rhs_scale=z_scales[:, lo:hi], start=True, stop=True,
+                )
+            if hi < N:
+                nc.scalar.activation(s[0][:, lo:hi], s_acc[0][:, lo:hi], COPY, scale=0.0625)
+        nc.scalar.activation(s[0][:, 384:N], s_acc[0][:, 384:N], COPY, scale=0.0625)
+        for t in range(PACK):
+            if t + 1 < PACK:
+                nc.scalar.activation(s[t + 1][:], s_acc[t + 1][:], COPY, scale=0.0625)
+            nc.scalar.activation(ds[t][:], s_acc[t][:], COPY, scale=0.0625)
+
+        pa = [keep.tile([P, HALF], F32, name="pa%d" % t) for t in range(PACK)]
+        pb = [keep.tile([P, HALF], F32, name="pb%d" % t) for t in range(PACK)]
+        hd = [keep.tile([P, N], F32, name="hd%d" % t) for t in range(PACK)]
+        res = [keep.tile([P, N], F32, name="res%d" % t) for t in range(PACK)]
+        out_rows = out.rearrange("(a t b) j -> t a b j", t=4, a=16)
+
+        def fetch(t):
+            nc.vector.tensor_copy(pa[t][:], s[t][:].indirect(n3_sb[:]))
+            nc.vector.tensor_scalar(pb[t][:], s[t][:].indirect(n4_sb[:]), -0.5, 0.0, MULT, ADD)
+
+        def put(t):
+            nc.vector.tensor_tensor(ds[t][:].indirect(n4_sb[:]), pa[t][:], pb[t][:], ADD)
+            nc.scalar.activation(hd[t][:], ds[t][:], COPY, scale=-0.5)
+
+        def finish(t):
+            for lo, hi in halves:
+                nc.vector.tensor_tensor(res[t][:, lo:hi], hd[t][:].indirect(n5_sb[:, cols16(lo, hi)]), ds[t][:, lo:hi], ADD)
+                if t == PACK - 1:
+                    nc.sync.dma_start(out_rows[t][:, :, lo:hi], res[t][:, lo:hi])
+            if t < PACK - 1:
+                nc.sync.dma_start(out_rows[t], res[t][:])
+
+        fetch(0)
+        for t in range(PACK):
+            if t + 1 < PACK:
+                fetch(t + 1)
+            put(t)
+            if t > 0:
+                finish(t - 1)
+        finish(PACK - 1)

@@ -18,6 +18,7 @@ PACK = 4
 T = 2048
 N = 512
 HALF = 256
+WIDE = 1024
 FLOPS = 2 * 2 * 512 * 512 * 512
 
 
@@ -42,10 +43,10 @@ def tile_picked_candsumfoldd_none_p_kernel(tc, x_words, x_scales, w1, gs, offs, 
             rows = x_scales[0, 4 * q : 4 * q + 4, :].bitcast(I32)
             nc.sync.dma_start(xs[32 * q : 32 * q + 32, :].bitcast(I32), rows.unsqueeze(0).to_broadcast([8, 4, T // 4]))
         cand_sb = load_list("cand_sb", cand)
-        xw = keep.tile([P, T], I32, name="xw")
-        nc.sync.dma_start(xw[:], x_words[0].rearrange("p n t -> p (n t)").bitcast(I32))
         w_raw = keep.tile([P, PACK, N], F32, name="w_raw")
         nc.sync.dma_start(w_raw[:], w1.rearrange("(p j) c -> p j c", j=PACK))
+        xw = keep.tile([P, T], I32, name="xw")
+        nc.sync.dma_start(xw[:], x_words[0].rearrange("p n t -> p (n t)").bitcast(I32))
         gs_sb = keep.tile([P, PACK], F32, name="gs_sb")
         nc.sync.dma_start(gs_sb[:], gs.rearrange("(p t) o -> p (t o)", t=PACK))
         n2_sb = load_list("n2_sb", n2)
@@ -58,18 +59,6 @@ def tile_picked_candsumfoldd_none_p_kernel(tc, x_words, x_scales, w1, gs, offs, 
         nc.vector.tensor_copy(pick_scales[:], xs[:].indirect(offs_sb[:]))
         cand_scales_raw = keep.tile([P, N], U8, name="cand_scales_raw", align_bytes=64)
         nc.vector.tensor_copy(cand_scales_raw[:], xs[:].indirect(cand_sb[:]))
-        cand_scales = keep.tile([P, N], U8, name="cand_scales", align_bytes=64)
-        nc.vector.tensor_copy(
-            cand_scales[:].bitcast(I32).rearrange("p (t a b) -> p t a b", t=4, a=16),
-            cand_scales_raw[:].bitcast(I32).rearrange("p (a t b) -> p t a b", t=4, a=16),
-        )
-
-        pick_words = keep.tile([P, N], U32, name="pick_words", align_bytes=64)
-        nc.vector.tensor_copy(pick_words[:], xw[:].bitcast(U32).indirect(offs_sb[:]))
-        cand_words = keep.tile([P, N], U32, name="cand_words", align_bytes=64)
-        nc.vector.tensor_copy(
-            cand_words[:].rearrange("p (t a b) -> p a t b", t=4, a=16), xw[:].bitcast(U32).indirect(cand_sb[:])
-        )
 
         w_src = w_raw[:].rearrange("p j (m u e) -> p u m j e", u=2, e=2)
         w_codes, w_scales = [], []
@@ -78,6 +67,11 @@ def tile_picked_candsumfoldd_none_p_kernel(tc, x_words, x_scales, w1, gs, offs, 
             w_dst = w_bf[:].rearrange("p e m j -> p m j e")
             if u == 0:
                 nc.vector.tensor_copy(w_dst, w_src[:, u])
+                cand_scales = keep.tile([P, N], U8, name="cand_scales", align_bytes=64)
+                nc.vector.tensor_copy(
+                    cand_scales[:].bitcast(I32).rearrange("p (t a b) -> p t a b", t=4, a=16),
+                    cand_scales_raw[:].bitcast(I32).rearrange("p (a t b) -> p t a b", t=4, a=16),
+                )
             else:
                 nc.scalar.copy(w_dst, w_src[:, u])
             codes = keep.tile([P, HALF], U32, name="w_codes%d" % u, align_bytes=64)
@@ -86,96 +80,134 @@ def tile_picked_candsumfoldd_none_p_kernel(tc, x_words, x_scales, w1, gs, offs, 
             w_codes.append(codes)
             w_scales.append(scales)
 
-        gy = []
+        halves = [(0, 256), (256, 512)]
+        pieces = [(0, 256), (256, 384), (384, 512)]
+        pick_words = keep.tile([P, N], U32, name="pick_words", align_bytes=64)
+        for lo, hi in halves:
+            nc.vector.tensor_copy(pick_words[:, lo:hi], xw[:].bitcast(U32).indirect(offs_sb[:, cols16(lo, hi)]))
+        cand_words = keep.tile([P, N], U32, name="cand_words", align_bytes=64)
+        nc.vector.tensor_copy(
+            cand_words[:].rearrange("p (t a b) -> p a t b", t=4, a=16), xw[:].bitcast(U32).indirect(cand_sb[:])
+        )
+
+        y_acc = []
         for t in range(PACK):
-            acc = psum.tile([P, N], F32, name="y_acc%d" % t)
+            acc = psum.tile([P, N], F32, name="y_acc%d" % t, tag="bank%d" % t)
+            y_acc.append(acc)
+        far_window = [keep.tile([P, WIDE], F32, name="far_window%d" % t) for t in range(PACK)]
+        near_window = [keep.tile([P, WIDE if t < 2 else N], F32, name="near_window%d" % t) for t in range(PACK)]
+
+        def project(t, lo, hi):
             m = slice(P * (t % 2), P * (t % 2 + 1))
             nc.tensor.matmul_mx(
-                out=acc[:], lhsT=w_codes[t // 2][:, m].bitcast(FP8X4), lhsT_scale=w_scales[t // 2][:, m],
-                rhs=pick_words[:].bitcast(FP8X4), rhs_scale=pick_scales[:], start=True, stop=True,
+                out=y_acc[t][:, lo:hi], lhsT=w_codes[t // 2][:, m].bitcast(FP8X4), lhsT_scale=w_scales[t // 2][:, m],
+                rhs=pick_words[:, lo:hi].bitcast(FP8X4), rhs_scale=pick_scales[:, lo:hi], start=True, stop=True,
             )
-            g = keep.tile([P, N], F32, name="gy%d" % t)
-            nc.scalar.activation(g[:], acc[:], COPY, scale=gs_sb[:, t : t + 1])
-            gy.append(g)
 
-        z32 = keep.tile([P, PACK, N], F32, name="z32")
-        far = keep.tile([P, PACK, N], F32, name="far")
+        def fill(window, t, lo, hi):
+            nc.scalar.activation(window[t][:, lo:hi], y_acc[t][:, lo:hi], COPY, scale=gs_sb[:, t : t + 1])
+
+        for lo, hi in halves:
+            project(0, lo, hi)
+            fill(far_window, 0, lo, hi)
+        for t in (1, 3, 2):
+            project(t, 0, N)
+        for window, t in ((far_window, 1), (near_window, 0), (far_window, 3), (near_window, 1), (far_window, 2), (near_window, 3), (near_window, 2)):
+            fill(window, t, 0, N)
+
         z_bf = keep.tile([P, N, PACK], BF16, name="z_bf", align_bytes=64)
         z_codes = keep.tile([P, N], U32, name="z_codes", align_bytes=64)
         z_scales = keep.tile([P, N], U8, name="z_scales", align_bytes=64)
-        halves = [(0, 256), (256, 512)]
-        pieces = [(0, 256), (256, 384), (384, 512)]
+        far01 = keep.tile([P, 2, N], F32, name="far01")
+        z01 = keep.tile([P, 2, N], F32, name="z01")
+        slots = keep.tile([P, 7 * HALF], F32, name="slots")
+        far = [far01[:, 0, :], far01[:, 1, :], slots[:, HALF : 3 * HALF], slots[:, 3 * HALF : 5 * HALF]]
+        z23 = [
+            slots[:, 5 * HALF : 7 * HALF].rearrange("p (e j) -> p e j", e=2),
+            slots[:, 0 : 2 * HALF].rearrange("p (e j) -> p e j", e=2),
+        ]
 
-        def gather_far(t, lo, hi):
-            nc.vector.tensor_scalar(far[:, t, lo:hi], gy[t][:].indirect(n2_sb[:, cols16(lo, hi)]), 0.75, 0.0, MULT, ADD)
+        def gather_far(t):
+            nc.vector.tensor_scalar(far[t], far_window[t][:].indirect(n2_sb[:]), 0.75, 0.0, MULT, ADD)
 
-        def gather_near(t, lo, hi):
-            nc.vector.tensor_tensor(z32[:, t, lo:hi], gy[t][:].indirect(n1_sb[:, cols16(lo, hi)]), far[:, t, lo:hi], ADD)
+        def gather_near(dst, t, lo, hi):
+            nc.vector.tensor_tensor(dst, near_window[t][:].indirect(n1_sb[:, cols16(lo, hi)]), far[t][:, lo:hi], ADD)
 
-        def weave(u, lo, hi):
-            nc.scalar.copy(z_bf[:, lo:hi, 2 * u : 2 * u + 2], z32[:, 2 * u : 2 * u + 2, lo:hi].rearrange("p e j -> p j e"))
+        gather_far(0)
+        gather_far(1)
+        gather_near(z01[:, 0, :], 0, 0, N)
+        gather_far(3)
+        gather_near(z01[:, 1, :], 1, 0, N)
+        nc.scalar.copy(z_bf[:, :, 0:2], z01[:].rearrange("p e j -> p j e"))
+        gather_far(2)
+        gather_near(z23[0][:, 1, :], 3, 0, HALF)
+        gather_near(z23[0][:, 0, :], 2, 0, HALF)
+        nc.scalar.copy(z_bf[:, 0:HALF, 2:4], z23[0].rearrange("p e j -> p j e"))
+        gather_near(z23[1][:, 0, :], 2, HALF, N)
+        for lo, hi in pieces[1:]:
+            gather_near(z23[1][:, 1, lo - HALF : hi - HALF], 3, lo, hi)
+            nc.scalar.copy(z_bf[:, lo:hi, 2:4], z23[1][:, :, lo - HALF : hi - HALF].rearrange("p e j -> p j e"))
 
-        for t in range(PACK - 1):
-            for lo, hi in halves:
-                gather_far(t, lo, hi)
-            for lo, hi in halves:
-                gather_near(t, lo, hi)
-            if t == 1:
-                weave(0, 0, N)
-        for lo, hi in halves:
-            gather_far(3, lo, hi)
-        s_acc = [psum.tile([P, N], F32, name="s_acc%d" % t) for t in range(PACK)]
+        s_acc = [psum.tile([P, N], F32, name="s_acc%d" % t, tag="bank%d" % t) for t in range(PACK)]
+        s_last = psum.tile([P, P], F32, name="s_last", tag="bank7")
         s = [keep.tile([P, N], F32, name="s%d" % t) for t in range(PACK)]
         ds = [keep.tile([P, N], F32, name="ds%d" % t) for t in range(PACK)]
-        for lo, hi in pieces:
-            gather_near(3, lo, hi)
-            weave(1, lo, hi)
+
+        def score(dst, t, lo, hi):
+            m = slice(P * t, P * (t + 1))
+            nc.tensor.matmul_mx(
+                out=dst, lhsT=cand_words[:, m].bitcast(FP8X4), lhsT_scale=cand_scales[:, m],
+                rhs=z_codes[:, lo:hi].bitcast(FP8X4), rhs_scale=z_scales[:, lo:hi], start=True, stop=True,
+            )
+
         for lo, hi in pieces:
             nc.vector.quantize_mx(
                 out=z_codes[:, lo:hi].bitcast(FP8X4), scales=z_scales[:, lo:hi],
                 in_=z_bf[:, lo:hi, :].rearrange("p j t -> p (j t)"),
             )
-            for t in range(PACK):
-                m = slice(P * t, P * (t + 1))
-                nc.tensor.matmul_mx(
-                    out=s_acc[t][:, lo:hi], lhsT=cand_words[:, m].bitcast(FP8X4), lhsT_scale=cand_scales[:, m],
-                    rhs=z_codes[:, lo:hi].bitcast(FP8X4), rhs_scale=z_scales[:, lo:hi], start=True, stop=True,
-                )
-            if hi < N:
-                nc.scalar.activation(s[0][:, lo:hi], s_acc[0][:, lo:hi], COPY, scale=0.0625)
-        nc.scalar.activation(s[0][:, 384:N], s_acc[0][:, 384:N], COPY, scale=0.0625)
+            score(s_acc[0][:, lo:hi] if hi < N else s_last[:], 0, lo, hi)
+        for t in range(1, PACK):
+            score(s_acc[t][:], t, 0, N)
+
+        def evacuate(dst, t):
+            if t == 0:
+                nc.scalar.activation(dst[:, 0:384], s_acc[0][:, 0:384], COPY, scale=0.0625)
+                nc.scalar.activation(dst[:, 384:N], s_last[:], COPY, scale=0.0625)
+            else:
+                nc.scalar.activation(dst[:, 0:N], s_acc[t][:], COPY, scale=0.0625)
+
+        evacuate(s[0], 0)
         for t in range(PACK):
             if t + 1 < PACK:
-                nc.scalar.activation(s[t + 1][:], s_acc[t + 1][:], COPY, scale=0.0625)
-            nc.scalar.activation(ds[t][:], s_acc[t][:], COPY, scale=0.0625)
+                evacuate(s[t + 1], t + 1)
+            evacuate(ds[t], t)
 
-        pa = [keep.tile([P, HALF], F32, name="pa%d" % t) for t in range(PACK)]
-        pb = [keep.tile([P, HALF], F32, name="pb%d" % t) for t in range(PACK)]
-        hd = [keep.tile([P, N], F32, name="hd%d" % t) for t in range(PACK)]
-        res = [keep.tile([P, N], F32, name="res%d" % t) for t in range(PACK)]
+        pair = [keep.tile([P, N], F32, name="pair%d" % t) for t in range(PACK)]
         out_rows = out.rearrange("(a t b) j -> t a b j", t=4, a=16)
 
         def fetch(t):
-            nc.vector.tensor_copy(pa[t][:], s[t][:].indirect(n3_sb[:]))
-            nc.vector.tensor_scalar(pb[t][:], s[t][:].indirect(n4_sb[:]), -0.5, 0.0, MULT, ADD)
+            nc.vector.tensor_copy(pair[t][:, 0:HALF], s[t][:].indirect(n3_sb[:]))
+            nc.vector.tensor_scalar(pair[t][:, HALF:N], s[t][:].indirect(n4_sb[:]), -0.5, 0.0, MULT, ADD)
 
         def put(t):
-            nc.vector.tensor_tensor(ds[t][:].indirect(n4_sb[:]), pa[t][:], pb[t][:], ADD)
-            nc.scalar.activation(hd[t][:], ds[t][:], COPY, scale=-0.5)
+            nc.vector.tensor_tensor(ds[t][:].indirect(n4_sb[:]), pair[t][:, 0:HALF], pair[t][:, HALF:N], ADD)
 
-        def finish(t):
-            for lo, hi in halves:
-                nc.vector.tensor_tensor(res[t][:, lo:hi], hd[t][:].indirect(n5_sb[:, cols16(lo, hi)]), ds[t][:, lo:hi], ADD)
-                if t == PACK - 1:
-                    nc.sync.dma_start(out_rows[t][:, :, lo:hi], res[t][:, lo:hi])
-            if t < PACK - 1:
-                nc.sync.dma_start(out_rows[t], res[t][:])
+        def halve(t):
+            hd = keep.tile([P, WIDE if t + 1 < PACK else N], F32, name="hd%d" % t)
+            nc.scalar.activation(hd[:, 0:N], ds[t][:], COPY, scale=-0.5)
+            return hd
+
+        def finish(t, hd):
+            res = keep.tile([P, N], F32, name="res%d" % t)
+            for lo, hi in [(0, N)] if t + 1 < PACK else halves:
+                nc.vector.tensor_tensor(res[:, lo:hi], hd[:].indirect(n5_sb[:, cols16(lo, hi)]), ds[t][:, lo:hi], ADD)
+                nc.sync.dma_start(out_rows[t][:, :, lo:hi], res[:, lo:hi])
 
         fetch(0)
         for t in range(PACK):
             if t + 1 < PACK:
                 fetch(t + 1)
             put(t)
-            if t > 0:
-                finish(t - 1)
-        finish(PACK - 1)
+        halved = [halve(t) for t in range(PACK)]
+        for t in range(PACK):
+            finish(t, halved[t])

@@ -94,18 +94,22 @@ def tile_picked_candsumfoldd_none_p_kernel(tc, x_words, x_scales, w1, gs, offs, 
         for t in range(PACK):
             acc = psum.tile([P, N], F32, name="y_acc%d" % t, tag="bank%d" % t)
             y_acc.append(acc)
+        y_second = psum.tile([P, HALF], F32, name="y_second", tag="bank7")
         far_window = [keep.tile([P, WIDE], F32, name="far_window%d" % t) for t in range(PACK)]
         near_window = [keep.tile([P, WIDE if t < 2 else N], F32, name="near_window%d" % t) for t in range(PACK)]
+
+        def y_sums(t, lo, hi):
+            return y_second[:] if lo == HALF else y_acc[t][:, lo:hi]
 
         def project(t, lo, hi):
             m = slice(P * (t % 2), P * (t % 2 + 1))
             nc.tensor.matmul_mx(
-                out=y_acc[t][:, lo:hi], lhsT=w_codes[t // 2][:, m].bitcast(FP8X4), lhsT_scale=w_scales[t // 2][:, m],
+                out=y_sums(t, lo, hi), lhsT=w_codes[t // 2][:, m].bitcast(FP8X4), lhsT_scale=w_scales[t // 2][:, m],
                 rhs=pick_words[:, lo:hi].bitcast(FP8X4), rhs_scale=pick_scales[:, lo:hi], start=True, stop=True,
             )
 
         def fill(window, t, lo, hi):
-            nc.scalar.activation(window[t][:, lo:hi], y_acc[t][:, lo:hi], COPY, scale=gs_sb[:, t : t + 1])
+            nc.scalar.activation(window[t][:, lo:hi], y_sums(t, lo, hi), COPY, scale=gs_sb[:, t : t + 1])
 
         for lo, hi in halves:
             project(0, lo, hi)
@@ -113,7 +117,8 @@ def tile_picked_candsumfoldd_none_p_kernel(tc, x_words, x_scales, w1, gs, offs, 
         for t in (1, 3, 2):
             project(t, 0, N)
         for window, t in ((far_window, 1), (near_window, 0), (far_window, 3), (near_window, 1), (far_window, 2), (near_window, 3), (near_window, 2)):
-            fill(window, t, 0, N)
+            for lo, hi in halves if t == 0 else [(0, N)]:
+                fill(window, t, lo, hi)
 
         z_bf = keep.tile([P, N, PACK], BF16, name="z_bf", align_bytes=64)
         z_codes = keep.tile([P, N], U32, name="z_codes", align_bytes=64)
@@ -199,7 +204,7 @@ def tile_picked_candsumfoldd_none_p_kernel(tc, x_words, x_scales, w1, gs, offs, 
 
         def finish(t, hd):
             res = keep.tile([P, N], F32, name="res%d" % t)
-            for lo, hi in [(0, N)] if t + 1 < PACK else halves:
+            for lo, hi in [(0, N)] if t + 1 < PACK else pieces:
                 nc.vector.tensor_tensor(res[:, lo:hi], hd[:].indirect(n5_sb[:, cols16(lo, hi)]), ds[t][:, lo:hi], ADD)
                 nc.sync.dma_start(out_rows[t][:, :, lo:hi], res[:, lo:hi])
 

from contextlib import ExitStack

import concourse.mybir as mybir

F32 = mybir.dt.float32
BF16 = mybir.dt.bfloat16
I32 = mybir.dt.int32
U32 = mybir.dt.uint32
U16 = mybir.dt.uint16
U8 = mybir.dt.uint8
FP8X4 = mybir.dt.float8_e4m3fn_x4
MULT = mybir.AluOpType.mult
ADD = mybir.AluOpType.add
COPY = mybir.ActivationFunctionType.Copy

P = 128
PACK = 4
T = 2048
N = 512
HALF = 256
WIDE = 1024
FLOPS = 2 * 2 * 512 * 512 * 512


def cols16(lo, hi):
    return slice(lo // 16, hi // 16)


def tile_picked_candsumfoldd_none_p_kernel(tc, x_words, x_scales, w1, gs, offs, n1, n2, cand, n3, n4, n5, out):
    nc = tc.nc
    with ExitStack() as ctx:
        keep = ctx.enter_context(tc.tile_pool(name="keep", bufs=1))
        psum = ctx.enter_context(tc.psum_pool(name="psum", bufs=1))

        def load_list(name, src):
            tile = keep.tile(list(src.shape), U16, name=name)
            nc.sync.dma_start(tile[:], src)
            return tile

        xs = keep.tile([P, T], U8, name="xs")
        offs_sb = load_list("offs_sb", offs)
        for q in range(4):
            rows = x_scales[0, 4 * q : 4 * q + 4, :].bitcast(I32)
            nc.sync.dma_start(xs[32 * q : 32 * q + 32, :].bitcast(I32), rows.unsqueeze(0).to_broadcast([8, 4, T // 4]))
        cand_sb = load_list("cand_sb", cand)
        w_raw = keep.tile([P, PACK, N], F32, name="w_raw")
        nc.sync.dma_start(w_raw[:], w1.rearrange("(p j) c -> p j c", j=PACK))
        xw = keep.tile([P, T], I32, name="xw")
        nc.sync.dma_start(xw[:], x_words[0].rearrange("p n t -> p (n t)").bitcast(I32))
        gs_sb = keep.tile([P, PACK], F32, name="gs_sb")
        nc.sync.dma_start(gs_sb[:], gs.rearrange("(p t) o -> p (t o)", t=PACK))
        n2_sb = load_list("n2_sb", n2)
        n1_sb = load_list("n1_sb", n1)
        n3_sb = load_list("n3_sb", n3)
        n4_sb = load_list("n4_sb", n4)
        n5_sb = load_list("n5_sb", n5)

        pick_scales = keep.tile([P, N], U8, name="pick_scales", align_bytes=64)
        nc.vector.tensor_copy(pick_scales[:], xs[:].indirect(offs_sb[:]))
        cand_scales_raw = keep.tile([P, N], U8, name="cand_scales_raw", align_bytes=64)
        nc.vector.tensor_copy(cand_scales_raw[:], xs[:].indirect(cand_sb[:]))

        w_src = w_raw[:].rearrange("p j (m u e) -> p u m j e", u=2, e=2)
        w_codes, w_scales = [], []
        for u in range(2):
            w_bf = keep.tile([P, 2, P, PACK], BF16, name="w_bf%d" % u, align_bytes=64)
            w_dst = w_bf[:].rearrange("p e m j -> p m j e")
            if u == 0:
                nc.vector.tensor_copy(w_dst, w_src[:, u])
                cand_scales = keep.tile([P, N], U8, name="cand_scales", align_bytes=64)
                nc.vector.tensor_copy(
                    cand_scales[:].bitcast(I32).rearrange("p (t a b) -> p t a b", t=4, a=16),
                    cand_scales_raw[:].bitcast(I32).rearrange("p (a t b) -> p t a b", t=4, a=16),
                )
            else:
                nc.scalar.copy(w_dst, w_src[:, u])
            codes = keep.tile([P, HALF], U32, name="w_codes%d" % u, align_bytes=64)
            scales = keep.tile([P, HALF], U8, name="w_scales%d" % u, align_bytes=64)
            nc.vector.quantize_mx(out=codes[:].bitcast(FP8X4), scales=scales[:], in_=w_bf[:].rearrange("p e m j -> p (e m j)"))
            w_codes.append(codes)
            w_scales.append(scales)

        halves = [(0, 256), (256, 512)]
        pieces = [(0, 256), (256, 384), (384, 512)]
        pick_words = keep.tile([P, N], U32, name="pick_words", align_bytes=64)
        for lo, hi in halves:
            nc.vector.tensor_copy(pick_words[:, lo:hi], xw[:].bitcast(U32).indirect(offs_sb[:, cols16(lo, hi)]))
        cand_words = keep.tile([P, N], U32, name="cand_words", align_bytes=64)
        nc.vector.tensor_copy(
            cand_words[:].rearrange("p (t a b) -> p a t b", t=4, a=16), xw[:].bitcast(U32).indirect(cand_sb[:])
        )

        y_acc = []
        for t in range(PACK):
            acc = psum.tile([P, N], F32, name="y_acc%d" % t, tag="bank%d" % t)
            y_acc.append(acc)
        y_second = psum.tile([P, HALF], F32, name="y_second", tag="bank7")
        far_window = [keep.tile([P, WIDE], F32, name="far_window%d" % t) for t in range(PACK)]
        near_window = [keep.tile([P, WIDE if t < 2 else N], F32, name="near_window%d" % t) for t in range(PACK)]

        def y_sums(t, lo, hi):
            return y_second[:] if lo == HALF else y_acc[t][:, lo:hi]

        def project(t, lo, hi):
            m = slice(P * (t % 2), P * (t % 2 + 1))
            nc.tensor.matmul_mx(
                out=y_sums(t, lo, hi), lhsT=w_codes[t // 2][:, m].bitcast(FP8X4), lhsT_scale=w_scales[t // 2][:, m],
                rhs=pick_words[:, lo:hi].bitcast(FP8X4), rhs_scale=pick_scales[:, lo:hi], start=True, stop=True,
            )

        def fill(window, t, lo, hi):
            nc.scalar.activation(window[t][:, lo:hi], y_sums(t, lo, hi), COPY, scale=gs_sb[:, t : t + 1])

        for lo, hi in halves:
            project(0, lo, hi)
            fill(far_window, 0, lo, hi)
        for t in (1, 3, 2):
            project(t, 0, N)
        for window, t in ((far_window, 1), (near_window, 0), (far_window, 3), (near_window, 1), (far_window, 2), (near_window, 3), (near_window, 2)):
            for lo, hi in halves if t == 0 else [(0, N)]:
                fill(window, t, lo, hi)

        z_bf = keep.tile([P, N, PACK], BF16, name="z_bf", align_bytes=64)
        z_codes = keep.tile([P, N], U32, name="z_codes", align_bytes=64)
        z_scales = keep.tile([P, N], U8, name="z_scales", align_bytes=64)
        far01 = keep.tile([P, 2, N], F32, name="far01")
        z01 = keep.tile([P, 2, N], F32, name="z01")
        slots = keep.tile([P, 7 * HALF], F32, name="slots")
        far = [far01[:, 0, :], far01[:, 1, :], slots[:, HALF : 3 * HALF], slots[:, 3 * HALF : 5 * HALF]]
        z23 = [
            slots[:, 5 * HALF : 7 * HALF].rearrange("p (e j) -> p e j", e=2),
            slots[:, 0 : 2 * HALF].rearrange("p (e j) -> p e j", e=2),
        ]

        def gather_far(t):
            nc.vector.tensor_scalar(far[t], far_window[t][:].indirect(n2_sb[:]), 0.75, 0.0, MULT, ADD)

        def gather_near(dst, t, lo, hi):
            nc.vector.tensor_tensor(dst, near_window[t][:].indirect(n1_sb[:, cols16(lo, hi)]), far[t][:, lo:hi], ADD)

        gather_far(0)
        gather_far(1)
        gather_near(z01[:, 0, :], 0, 0, N)
        gather_far(3)
        gather_near(z01[:, 1, :], 1, 0, N)
        nc.scalar.copy(z_bf[:, :, 0:2], z01[:].rearrange("p e j -> p j e"))
        gather_far(2)
        gather_near(z23[0][:, 1, :], 3, 0, HALF)
        gather_near(z23[0][:, 0, :], 2, 0, HALF)
        nc.scalar.copy(z_bf[:, 0:HALF, 2:4], z23[0].rearrange("p e j -> p j e"))
        gather_near(z23[1][:, 0, :], 2, HALF, N)
        for lo, hi in pieces[1:]:
            gather_near(z23[1][:, 1, lo - HALF : hi - HALF], 3, lo, hi)
            nc.scalar.copy(z_bf[:, lo:hi, 2:4], z23[1][:, :, lo - HALF : hi - HALF].rearrange("p e j -> p j e"))

        s_acc = [psum.tile([P, N], F32, name="s_acc%d" % t, tag="bank%d" % t) for t in range(PACK)]
        s_last = psum.tile([P, P], F32, name="s_last", tag="bank7")
        s = [keep.tile([P, N], F32, name="s%d" % t) for t in range(PACK)]
        ds = [keep.tile([P, N], F32, name="ds%d" % t) for t in range(PACK)]

        def score(dst, t, lo, hi):
            m = slice(P * t, P * (t + 1))
            nc.tensor.matmul_mx(
                out=dst, lhsT=cand_words[:, m].bitcast(FP8X4), lhsT_scale=cand_scales[:, m],
                rhs=z_codes[:, lo:hi].bitcast(FP8X4), rhs_scale=z_scales[:, lo:hi], start=True, stop=True,
            )

        for lo, hi in pieces:
            nc.vector.quantize_mx(
                out=z_codes[:, lo:hi].bitcast(FP8X4), scales=z_scales[:, lo:hi],
                in_=z_bf[:, lo:hi, :].rearrange("p j t -> p (j t)"),
            )
            score(s_acc[0][:, lo:hi] if hi < N else s_last[:], 0, lo, hi)
        for t in range(1, PACK):
            score(s_acc[t][:], t, 0, N)

        def evacuate(dst, t):
            if t == 0:
                nc.scalar.activation(dst[:, 0:384], s_acc[0][:, 0:384], COPY, scale=0.0625)
                nc.scalar.activation(dst[:, 384:N], s_last[:], COPY, scale=0.0625)
            else:
                nc.scalar.activation(dst[:, 0:N], s_acc[t][:], COPY, scale=0.0625)

        evacuate(s[0], 0)
        for t in range(PACK):
            if t + 1 < PACK:
                evacuate(s[t + 1], t + 1)
            evacuate(ds[t], t)

        pair = [keep.tile([P, N], F32, name="pair%d" % t) for t in range(PACK)]
        out_rows = out.rearrange("(a t b) j -> t a b j", t=4, a=16)

        def fetch(t):
            nc.vector.tensor_copy(pair[t][:, 0:HALF], s[t][:].indirect(n3_sb[:]))
            nc.vector.tensor_scalar(pair[t][:, HALF:N], s[t][:].indirect(n4_sb[:]), -0.5, 0.0, MULT, ADD)

        def put(t):
            nc.vector.tensor_tensor(ds[t][:].indirect(n4_sb[:]), pair[t][:, 0:HALF], pair[t][:, HALF:N], ADD)

        def halve(t):
            hd = keep.tile([P, WIDE if t + 1 < PACK else N], F32, name="hd%d" % t)
            nc.scalar.activation(hd[:, 0:N], ds[t][:], COPY, scale=-0.5)
            return hd

        def finish(t, hd):
            res = keep.tile([P, N], F32, name="res%d" % t)
            for lo, hi in [(0, N)] if t + 1 < PACK else pieces:
                nc.vector.tensor_tensor(res[:, lo:hi], hd[:].indirect(n5_sb[:, cols16(lo, hi)]), ds[t][:, lo:hi], ADD)
                nc.sync.dma_start(out_rows[t][:, :, lo:hi], res[:, lo:hi])

        fetch(0)
        for t in range(PACK):
            if t + 1 < PACK:
                fetch(t + 1)
            put(t)
        halved = [halve(t) for t in range(PACK)]
        for t in range(PACK):
            finish(t, halved[t])
